import numpy as np, ml_dtypes
CORES = [21,29,37,45,53,61,69,77,85]
N = 9
CB = 1
def setup_inputs(rng):
    k = (rng.standard_normal((N, 128, CB * 128), dtype=np.float32) / 8).astype(ml_dtypes.bfloat16)
    kt = np.concatenate([k[:, :, 128 * c:128 * c + 128].transpose(0, 2, 1) for c in range(CB)], axis=2)
    tri = np.triu(np.ones((128, 128), np.float32)).astype(ml_dtypes.bfloat16)
    return {"q": (rng.standard_normal((N, 128, CB * 128), dtype=np.float32) / 8).astype(ml_dtypes.bfloat16), "k": k, "kt": kt, "v": rng.standard_normal((N, 128, CB * 128), dtype=np.float32).astype(ml_dtypes.bfloat16), "m": np.broadcast_to(tri, (N, 128, 128)).copy()}
def setup_inputs_big(rng):
    d = setup_inputs(rng)
    for k in ("q", "k", "kt", "v"): d[k] = (d[k].astype(np.float32) * 1024.0).astype(d[k].dtype)
    return d
def setup_inputs_small(rng):
    d = setup_inputs(rng)
    for k in ("q", "k", "kt", "v"): d[k] = (d[k].astype(np.float32) * (1 / 1024.0)).astype(d[k].dtype)
    return d
def setup_inputs_apart(rng):
    d = setup_inputs(rng)
    f = (10.0 ** rng.permutation(np.linspace(-1.5, 1.5, N))).astype(np.float32).reshape(N, 1, 1)
    for k in ("q", "k", "kt", "v"): d[k] = (d[k].astype(np.float32) * f).astype(d[k].dtype)
    return d
def reference(q, k, kt, v, m):
    Q, K, KT, V, M = q.astype(np.float64), k.astype(np.float64), kt.astype(np.float64), v.astype(np.float64), m.astype(np.float64)
    y = np.zeros((N, 128, CB * 128)); Z = np.zeros((128, 128))
    for r in range(N):
        for c in range(CB):
            s = slice(128 * c, 128 * c + 128)
            y[r][:, s] = Z.T @ Q[r][:, s] + V[r][:, s].T @ ((K[r][:, s].T @ Q[r][:, s]) * M[r])
            Z = Z + KT[r][:, s].T @ V[r][:, s]
    return {"y": y.astype(ml_dtypes.bfloat16)}

@@ -1,0 +1,156 @@
+from concourse.bass import DstId, RemoteDMATransfer
+from concourse.mybir import AluOpType
+
+P = 128
+NR = 9
+RELAYS = 2
+ENG_RELAY_IN = 8
+ENG_RELAY_OUT = 8
+ENG_DIRECT = 8
+
+_BF = "bfloat16"
+SCRATCH = {
+    "kt_s": ("sbuf", [P, P], _BF), "v_s": ("sbuf", [P, P], _BF), "k_s": ("sbuf", [P, P], _BF),
+    "q_s": ("sbuf", [P, P], _BF), "m_s": ("sbuf", [P, P], _BF),
+    "s_b": ("sbuf", [P, P], _BF),
+    "am_b": ("sbuf", [P, P], _BF),
+    "y_b": ("sbuf", [P, P], _BF),
+    "relay": ("sbuf", [P, P], _BF),
+    "ps_s": ("psum", [P, 512], "float32"), "ps_a": ("psum", [P, 512], "float32"), "ps_y": ("psum", [P, 512], "float32"),
+}
+for _s in range(NR - 1):
+    SCRATCH["land%d" % _s] = ("sbuf", [P, P], _BF)
+
+SEMAPHORES = ["ld_kt", "ld_v", "ld_k", "ld_q", "ld_m", "mm_s", "cp_s", "mm_a", "cp_a", "mm_y", "cp_y", "st_y",
+              "sent", "hin"] + ["arr%d" % _s for _s in range(NR - 1)]
+
+
+def _bits(mask):
+    return [1 << b for b in range(mask.bit_length()) if (mask >> b) & 1]
+
+
+def _common_mask(topo, src, dsts):
+    m = topo.mask(src, dsts[0])
+    for d in dsts[1:]:
+        m &= topo.mask(src, d)
+    return m
+
+
+def _plan(T, topo):
+    cores = list(T.cores)
+    everyone = range(topo.CORES_PER_CHIP * topo.CHIPS)
+    plan = []
+    for s, c in enumerate(cores):
+        later = range(s + 1, len(cores))
+        direct = [r for r in later if topo.may_write(c, cores[r])]
+        cross = [r for r in later if not topo.may_write(c, cores[r])]
+        cand = [x for x in everyone
+                if topo.chip(x) == topo.chip(c) and x not in cores
+                and all(topo.may_write(x, cores[r]) for r in cross)]
+        cand.sort(key=lambda x: (topo.die(x) != topo.die(c), x))
+        nh = min(RELAYS, len(cross))
+        plan.append((direct, [(cand[i], cross[i::nh]) for i in range(nh)]))
+    return plan
+
+
+def _copy(topo, T, src_ap, dst_name, sem, dst_cores, mask):
+    ids = []
+    for d in dst_cores:
+        rid, pid, _ = topo.addr(d)
+        ids.append(DstId(rid=rid, pnc=pid))
+    return RemoteDMATransfer(dst_ids=ids, dma_engine_mask=mask, remote_sem=sem, srcs=[src_ap],
+                             dsts=[T[dst_name][:] for _ in dst_cores], alu_op=0)
+
+
+def _relay_in_bits(topo, cores, c, direct, relays):
+    on = _common_mask(topo, c, [h for h, _ in relays])
+    off = _common_mask(topo, c, [cores[r] for r in direct]) if direct else 0
+    b = [x for x in _bits(on) if not x & off] + [x for x in _bits(on) if x & off]
+    return b[:ENG_RELAY_IN]
+
+
+def rank_program(g, core, T, topo):
+    cores = list(T.cores)
+    plan = _plan(T, topo)
+    rank = T.rank_of(core)
+    sem = T.sem
+
+    if rank is None:
+        for s, (direct, relays) in enumerate(plan):
+            for h, served in relays:
+                if h != core:
+                    continue
+                n_in = len(_relay_in_bits(topo, cores, cores[s], direct, relays))
+                dst = [cores[r] for r in served]
+                out = _bits(_common_mask(topo, core, dst))[:ENG_RELAY_OUT]
+                g.wait_ge(sem.hin, n_in)
+                g.remote_dma_fused([_copy(topo, T, T.relay[:], "land%d" % s, sem["arr%d" % s], dst, sum(out))],
+                                   local_sem=sem.sent)
+                g.wait_ge(sem.sent, len(out))
+        return
+
+    direct, relays = plan[rank]
+    sends = bool(direct or relays)
+
+    if sends:
+        g.sync.dma_start(T.kt_s[:], T.kt[:]).then_inc(sem.ld_kt, 16)
+    g.scalar.dma_start(T.v_s[:], T.v[:]).then_inc(sem.ld_v, 16)
+    g.sync.dma_start(T.k_s[:], T.k[:]).then_inc(sem.ld_k, 16)
+    g.scalar.dma_start(T.q_s[:], T.q[:]).then_inc(sem.ld_q, 16)
+    g.sync.dma_start(T.m_s[:], T.m[:]).then_inc(sem.ld_m, 16)
+
+    ps_s, ps_a, ps_y = T.ps_s[:, 0:P], T.ps_a[:, 0:P], T.ps_y[:, 0:P]
+
+    g.tensor.wait_ge(sem.ld_v, 16)
+    if sends:
+        g.tensor.wait_ge(sem.ld_kt, 16)
+        g.tensor.matmul(ps_s, T.kt_s[:], T.v_s[:], True, True).then_inc(sem.mm_s, 1)
+        g.vector.wait_ge(sem.mm_s, 1)
+        g.vector.tensor_copy(T.s_b[:], ps_s).then_inc(sem.cp_s, 1)
+        g.wait_ge(sem.cp_s, 1)
+        left = 0
+        if relays:
+            b = _relay_in_bits(topo, cores, core, direct, relays)
+            g.remote_dma_fused([_copy(topo, T, T.s_b[:], "relay", sem.hin, [h for h, _ in relays], sum(b))],
+                               local_sem=sem.sent)
+            left += len(b)
+        if direct:
+            dst = [cores[r] for r in direct]
+            b = _bits(_common_mask(topo, core, dst))[:ENG_DIRECT]
+            g.remote_dma_fused([_copy(topo, T, T.s_b[:], "land%d" % rank, sem["arr%d" % rank], dst, sum(b))],
+                               local_sem=sem.sent)
+            left += len(b)
+        g.wait_ge(sem.sent, left)
+
+    g.tensor.wait_ge(sem.ld_k, 16)
+    g.tensor.wait_ge(sem.ld_q, 16)
+    g.tensor.matmul(ps_a, T.k_s[:], T.q_s[:], True, True).then_inc(sem.mm_a, 1)
+    g.vector.wait_ge(sem.mm_a, 1)
+    g.vector.wait_ge(sem.ld_m, 16)
+    g.vector.tensor_tensor(T.am_b[:], ps_a, T.m_s[:], AluOpType.mult).then_inc(sem.cp_a, 1)
+    g.tensor.wait_ge(sem.cp_a, 1)
+
+    came = []
+    for s in range(rank):
+        d_s, r_s = plan[s]
+        if rank in d_s:
+            n = len(_bits(_common_mask(topo, cores[s], [cores[r] for r in d_s]))[:ENG_DIRECT])
+            came.append((0, -s, s, n))
+        else:
+            for h, served in r_s:
+                if rank in served:
+                    n = len(_bits(_common_mask(topo, h, [cores[r] for r in served]))[:ENG_RELAY_OUT])
+                    came.append((1, -s, s, n))
+    came.sort()
+
+    mm = g.tensor.matmul(ps_y, T.v_s[:], T.am_b[:], True, not came)
+    for i, (_, _, s, n) in enumerate(came):
+        g.tensor.wait_ge(sem["arr%d" % s], n)
+        mm = g.tensor.matmul(ps_y, T["land%d" % s][:], T.q_s[:], False, i == len(came) - 1)
+    mm.then_inc(sem.mm_y, 1)
+
+    g.vector.wait_ge(sem.mm_y, 1)
+    g.vector.tensor_copy(T.y_b[:], ps_y).then_inc(sem.cp_y, 1)
+    g.sync.wait_ge(sem.cp_y, 1)
+    g.sync.dma_start(T.y[:], T.y_b[:]).then_inc(sem.st_y, 16)
+    g.sync.wait_ge(sem.st_y, 16)

@@ -1,12 +1,10 @@
 from concourse.bass import DstId, RemoteDMATransfer
-from concourse.mybir import AluOpType
+from concourse.mybir import AluOpType, ActivationFunctionType
 
 P = 128
+H = 64
 NR = 9
-RELAYS = 2
-ENG_RELAY_IN = 8
-ENG_RELAY_OUT = 8
-ENG_DIRECT = 8
+ENG = 8
 
 _BF = "bfloat16"
 SCRATCH = {
@@ -14,15 +12,19 @@ SCRATCH = {
     "q_s": ("sbuf", [P, P], _BF), "m_s": ("sbuf", [P, P], _BF),
     "s_b": ("sbuf", [P, P], _BF),
     "am_b": ("sbuf", [P, P], _BF),
+    "ar_b": ("sbuf", [P, P], _BF),
     "y_b": ("sbuf", [P, P], _BF),
-    "relay": ("sbuf", [P, P], _BF),
-    "ps_s": ("psum", [P, 512], "float32"), "ps_a": ("psum", [P, 512], "float32"), "ps_y": ("psum", [P, 512], "float32"),
+    "relay": ("sbuf", [P, P], _BF), "rl_k": ("sbuf", [P, P], _BF), "rl_v": ("sbuf", [P, P], _BF),
+    "rk": ("sbuf", [P, P], _BF), "rv": ("sbuf", [P, P], _BF),
+    "ps_s": ("psum", [P, 512], "float32"), "ps_a": ("psum", [P, 512], "float32"), "ps_r": ("psum", [P, 512], "float32"),
+    "ps_y0": ("psum", [P, 512], "float32"), "ps_y1": ("psum", [P, 512], "float32"),
 }
 for _s in range(NR - 1):
     SCRATCH["land%d" % _s] = ("sbuf", [P, P], _BF)
 
-SEMAPHORES = ["ld_kt", "ld_v", "ld_k", "ld_q", "ld_m", "mm_s", "cp_s", "mm_a", "cp_a", "mm_y", "cp_y", "st_y",
-              "sent", "hin"] + ["arr%d" % _s for _s in range(NR - 1)]
+SEMAPHORES = ["ld_kt", "ld_v", "ld_k", "ld_q", "ld_m", "mm_s", "cp_s", "mm_a", "cp_a", "mm_r", "cp_r",
+              "mm_y0", "mm_y1", "cp_y0", "cp_y1", "st_y", "sent", "hk", "hv", "hs", "ark", "arv"] \
+             + ["arr%d" % _s for _s in range(NR - 1)]
 
 
 def _bits(mask):
@@ -48,8 +50,18 @@ def _plan(T, topo):
                 if topo.chip(x) == topo.chip(c) and x not in cores
                 and all(topo.may_write(x, cores[r]) for r in cross)]
         cand.sort(key=lambda x: (topo.die(x) != topo.die(c), x))
-        nh = min(RELAYS, len(cross))
-        plan.append((direct, [(cand[i], cross[i::nh]) for i in range(nh)]))
+        if len(cross) >= 2:
+            rest = cross[1:]
+            if len(rest) == 3:
+                order = [rest[1], rest[2], rest[0]]
+            elif len(rest) == 2:
+                order = [rest[1], rest[0]]
+            else:
+                order = rest
+            srel = [(cand[1 + i], r) for i, r in enumerate(order)]
+            plan.append({"direct": direct, "raw": (cand[0], cross[0]), "srel": srel})
+        else:
+            plan.append({"direct": direct, "raw": None, "srel": [(cand[0], cross[0])] if cross else []})
     return plan
 
 
@@ -62,11 +74,15 @@ def _copy(topo, T, src_ap, dst_name, sem, dst_cores, mask):
                              dsts=[T[dst_name][:] for _ in dst_cores], alu_op=0)
 
 
-def _relay_in_bits(topo, cores, c, direct, relays):
-    on = _common_mask(topo, c, [h for h, _ in relays])
-    off = _common_mask(topo, c, [cores[r] for r in direct]) if direct else 0
+def _on_chip_masks(topo, cores, c, relay):
+    on = topo.mask(c, relay)
+    off = _common_mask(topo, c, [x for x in cores if x != c])
     b = [x for x in _bits(on) if not x & off] + [x for x in _bits(on) if x & off]
-    return b[:ENG_RELAY_IN]
+    return sum(b[:ENG]), sum(b[ENG:2 * ENG])
+
+
+def _off_chip_mask(topo, c, dsts):
+    return sum(_bits(_common_mask(topo, c, dsts))[:ENG])
 
 
 def rank_program(g, core, T, topo):
@@ -75,31 +91,45 @@ def rank_program(g, core, T, topo):
     rank = T.rank_of(core)
     sem = T.sem
 
+    def send(src, name, rsem, dsts, mask):
+        g.remote_dma_fused([_copy(topo, T, src, name, rsem, dsts, mask)], local_sem=sem.sent)
+
     if rank is None:
-        for s, (direct, relays) in enumerate(plan):
-            for h, served in relays:
-                if h != core:
-                    continue
-                n_in = len(_relay_in_bits(topo, cores, cores[s], direct, relays))
-                dst = [cores[r] for r in served]
-                out = _bits(_common_mask(topo, core, dst))[:ENG_RELAY_OUT]
-                g.wait_ge(sem.hin, n_in)
-                g.remote_dma_fused([_copy(topo, T, T.relay[:], "land%d" % s, sem["arr%d" % s], dst, sum(out))],
-                                   local_sem=sem.sent)
-                g.wait_ge(sem.sent, len(out))
+        left = 0
+        for s, p in enumerate(plan):
+            if p["raw"] and p["raw"][0] == core:
+                nxt = [cores[p["raw"][1]]]
+                mk = _off_chip_mask(topo, core, nxt)
+                g.wait_ge(sem.hk, ENG)
+                send(T.rl_k[:], "rk", sem.ark, nxt, mk)
+                g.wait_ge(sem.hv, ENG)
+                send(T.rl_v[:], "rv", sem.arv, nxt, mk)
+                left += 2 * ENG
+            for h, r in p["srel"]:
+                if h == core:
+                    dst = [cores[r]]
+                    g.wait_ge(sem.hs, ENG)
+                    send(T.relay[:], "land%d" % s, sem["arr%d" % s], dst, _off_chip_mask(topo, core, dst))
+                    left += ENG
+        if left:
+            g.wait_ge(sem.sent, left)
         return
 
-    direct, relays = plan[rank]
-    sends = bool(direct or relays)
+    p = plan[rank]
+    direct, raw, srel = p["direct"], p["raw"], p["srel"]
+    sends = bool(direct or srel)
 
+    if raw:
+        g.sync.dma_start(T.k_s[:], T.k[:]).then_inc(sem.ld_k, 16)
     if sends:
         g.sync.dma_start(T.kt_s[:], T.kt[:]).then_inc(sem.ld_kt, 16)
     g.scalar.dma_start(T.v_s[:], T.v[:]).then_inc(sem.ld_v, 16)
-    g.sync.dma_start(T.k_s[:], T.k[:]).then_inc(sem.ld_k, 16)
+    if not raw:
+        g.sync.dma_start(T.k_s[:], T.k[:]).then_inc(sem.ld_k, 16)
     g.scalar.dma_start(T.q_s[:], T.q[:]).then_inc(sem.ld_q, 16)
     g.sync.dma_start(T.m_s[:], T.m[:]).then_inc(sem.ld_m, 16)
 
-    ps_s, ps_a, ps_y = T.ps_s[:, 0:P], T.ps_a[:, 0:P], T.ps_y[:, 0:P]
+    ps_s, ps_a, ps_r = T.ps_s[:, 0:P], T.ps_a[:, 0:P], T.ps_r[:, 0:P]
 
     g.tensor.wait_ge(sem.ld_v, 16)
     if sends:
@@ -107,19 +137,28 @@ def rank_program(g, core, T, topo):
         g.tensor.matmul(ps_s, T.kt_s[:], T.v_s[:], True, True).then_inc(sem.mm_s, 1)
         g.vector.wait_ge(sem.mm_s, 1)
         g.vector.tensor_copy(T.s_b[:], ps_s).then_inc(sem.cp_s, 1)
+
+    left = 0
+    if sends:
+        hi, lo = _on_chip_masks(topo, cores, core, srel[0][0])
+        if raw:
+            g.wait_ge(sem.ld_k, 16)
+            send(T.k_s[:], "rl_k", sem.hk, [raw[0]], hi)
+            left += ENG
         g.wait_ge(sem.cp_s, 1)
-        left = 0
-        if relays:
-            b = _relay_in_bits(topo, cores, core, direct, relays)
-            g.remote_dma_fused([_copy(topo, T, T.s_b[:], "relay", sem.hin, [h for h, _ in relays], sum(b))],
-                               local_sem=sem.sent)
-            left += len(b)
+        feeds = [_copy(topo, T, T.s_b[:], "relay", sem.hs, [srel[0][0]], hi)]
+        if srel[1:]:
+            feeds.append(_copy(topo, T, T.s_b[:], "relay", sem.hs, [h for h, _ in srel[1:]], lo))
+        g.remote_dma_fused(feeds, local_sem=sem.sent)
+        left += ENG * len(feeds)
+        if raw:
+            g.wait_ge(sem.ld_v, 16)
+            send(T.v_s[:], "rl_v", sem.hv, [raw[0]], hi)
+            left += ENG
         if direct:
             dst = [cores[r] for r in direct]
-            b = _bits(_common_mask(topo, core, dst))[:ENG_DIRECT]
-            g.remote_dma_fused([_copy(topo, T, T.s_b[:], "land%d" % rank, sem["arr%d" % rank], dst, sum(b))],
-                               local_sem=sem.sent)
-            left += len(b)
+            send(T.s_b[:], "land%d" % rank, sem["arr%d" % rank], dst, _off_chip_mask(topo, core, dst))
+            left += ENG
         g.wait_ge(sem.sent, left)
 
     g.tensor.wait_ge(sem.ld_k, 16)
@@ -132,25 +171,48 @@ def rank_program(g, core, T, topo):
 
     came = []
     for s in range(rank):
-        d_s, r_s = plan[s]
-        if rank in d_s:
-            n = len(_bits(_common_mask(topo, cores[s], [cores[r] for r in d_s]))[:ENG_DIRECT])
-            came.append((0, -s, s, n))
-        else:
-            for h, served in r_s:
-                if rank in served:
-                    n = len(_bits(_common_mask(topo, h, [cores[r] for r in served]))[:ENG_RELAY_OUT])
-                    came.append((1, -s, s, n))
+        ps = plan[s]
+        if rank in ps["direct"]:
+            came.append((ps["direct"].index(rank), "S", s))
+        if ps["raw"] and ps["raw"][1] == rank:
+            came.append((102, "K", s))
+            came.append((103.5, "V", s))
+        for i, (h, r) in enumerate(ps["srel"]):
+            if r == rank:
+                came.append(((102.5 if not ps["raw"] else (103, 102.7, 103.2)[i]), "S", s))
     came.sort()
+    n_y = sum(1 for e in came if e[1] != "K")
 
-    mm = g.tensor.matmul(ps_y, T.v_s[:], T.am_b[:], True, not came)
-    for i, (_, _, s, n) in enumerate(came):
-        g.tensor.wait_ge(sem["arr%d" % s], n)
-        mm = g.tensor.matmul(ps_y, T["land%d" % s][:], T.q_s[:], False, i == len(came) - 1)
-    mm.then_inc(sem.mm_y, 1)
+    def ymm(lhsT, rhs, start, stop):
+        a = g.tensor.matmul(T.ps_y0[:, 0:H], lhsT, rhs[:, 0:H], start, stop)
+        b = g.tensor.matmul(T.ps_y1[:, 0:H], lhsT, rhs[:, H:P], start, stop)
+        if stop:
+            a.then_inc(sem.mm_y0, 1)
+            b.then_inc(sem.mm_y1, 1)
 
-    g.vector.wait_ge(sem.mm_y, 1)
-    g.vector.tensor_copy(T.y_b[:], ps_y).then_inc(sem.cp_y, 1)
-    g.sync.wait_ge(sem.cp_y, 1)
+    ymm(T.v_s[:], T.am_b, True, n_y == 0)
+    done = 0
+    for _, kind, s in came:
+        if kind == "K":
+            g.tensor.wait_ge(sem.ark, ENG)
+            g.tensor.matmul(ps_r, T.rk[:], T.q_s[:], True, True).then_inc(sem.mm_r, 1)
+            g.vector.wait_ge(sem.mm_r, 1)
+            g.vector.tensor_copy(T.ar_b[:], ps_r).then_inc(sem.cp_r, 1)
+            continue
+        done += 1
+        if kind == "V":
+            g.tensor.wait_ge(sem.cp_r, 1)
+            g.tensor.wait_ge(sem.arv, ENG)
+            ymm(T.rv[:], T.ar_b, False, done == n_y)
+        else:
+            g.tensor.wait_ge(sem["arr%d" % s], ENG)
+            ymm(T["land%d" % s][:], T.q_s, False, done == n_y)
+
+    g.scalar.wait_ge(sem.mm_y0, 1)
+    g.scalar.activation(T.y_b[:, 0:H], T.ps_y0[:, 0:H], ActivationFunctionType.Copy).then_inc(sem.cp_y0, 1)
+    g.vector.wait_ge(sem.mm_y1, 1)
+    g.vector.tensor_copy(T.y_b[:, H:P], T.ps_y1[:, 0:H]).then_inc(sem.cp_y1, 1)
+    g.sync.wait_ge(sem.cp_y0, 1)
+    g.sync.wait_ge(sem.cp_y1, 1)
     g.sync.dma_start(T.y[:], T.y_b[:]).then_inc(sem.st_y, 16)
     g.sync.wait_ge(sem.st_y, 16)

from concourse.bass import DstId, RemoteDMATransfer
from concourse.mybir import AluOpType, ActivationFunctionType

P = 128
H = 64
NR = 9
ENG = 8

_BF = "bfloat16"
SCRATCH = {
    "kt_s": ("sbuf", [P, P], _BF), "v_s": ("sbuf", [P, P], _BF), "k_s": ("sbuf", [P, P], _BF),
    "q_s": ("sbuf", [P, P], _BF), "m_s": ("sbuf", [P, P], _BF),
    "s_b": ("sbuf", [P, P], _BF),
    "am_b": ("sbuf", [P, P], _BF),
    "ar_b": ("sbuf", [P, P], _BF),
    "y_b": ("sbuf", [P, P], _BF),
    "relay": ("sbuf", [P, P], _BF), "rl_k": ("sbuf", [P, P], _BF), "rl_v": ("sbuf", [P, P], _BF),
    "rk": ("sbuf", [P, P], _BF), "rv": ("sbuf", [P, P], _BF),
    "ps_s": ("psum", [P, 512], "float32"), "ps_a": ("psum", [P, 512], "float32"), "ps_r": ("psum", [P, 512], "float32"),
    "ps_y0": ("psum", [P, 512], "float32"), "ps_y1": ("psum", [P, 512], "float32"),
}
for _s in range(NR - 1):
    SCRATCH["land%d" % _s] = ("sbuf", [P, P], _BF)

SEMAPHORES = ["ld_kt", "ld_v", "ld_k", "ld_q", "ld_m", "mm_s", "cp_s", "mm_a", "cp_a", "mm_r", "cp_r",
              "mm_y0", "mm_y1", "cp_y0", "cp_y1", "st_y", "sent", "hk", "hv", "hs", "ark", "arv"] \
             + ["arr%d" % _s for _s in range(NR - 1)]


def _bits(mask):
    return [1 << b for b in range(mask.bit_length()) if (mask >> b) & 1]


def _common_mask(topo, src, dsts):
    m = topo.mask(src, dsts[0])
    for d in dsts[1:]:
        m &= topo.mask(src, d)
    return m


def _plan(T, topo):
    cores = list(T.cores)
    everyone = range(topo.CORES_PER_CHIP * topo.CHIPS)
    plan = []
    for s, c in enumerate(cores):
        later = range(s + 1, len(cores))
        direct = [r for r in later if topo.may_write(c, cores[r])]
        cross = [r for r in later if not topo.may_write(c, cores[r])]
        cand = [x for x in everyone
                if topo.chip(x) == topo.chip(c) and x not in cores
                and all(topo.may_write(x, cores[r]) for r in cross)]
        cand.sort(key=lambda x: (topo.die(x) != topo.die(c), x))
        if len(cross) >= 2:
            rest = cross[1:]
            if len(rest) == 3:
                order = [rest[1], rest[2], rest[0]]
            elif len(rest) == 2:
                order = [rest[1], rest[0]]
            else:
                order = rest
            srel = [(cand[1 + i], r) for i, r in enumerate(order)]
            plan.append({"direct": direct, "raw": (cand[0], cross[0]), "srel": srel})
        else:
            plan.append({"direct": direct, "raw": None, "srel": [(cand[0], cross[0])] if cross else []})
    return plan


def _copy(topo, T, src_ap, dst_name, sem, dst_cores, mask):
    ids = []
    for d in dst_cores:
        rid, pid, _ = topo.addr(d)
        ids.append(DstId(rid=rid, pnc=pid))
    return RemoteDMATransfer(dst_ids=ids, dma_engine_mask=mask, remote_sem=sem, srcs=[src_ap],
                             dsts=[T[dst_name][:] for _ in dst_cores], alu_op=0)


def _on_chip_masks(topo, cores, c, relay):
    on = topo.mask(c, relay)
    off = _common_mask(topo, c, [x for x in cores if x != c])
    b = [x for x in _bits(on) if not x & off] + [x for x in _bits(on) if x & off]
    return sum(b[:ENG]), sum(b[ENG:2 * ENG])


def _off_chip_mask(topo, c, dsts):
    return sum(_bits(_common_mask(topo, c, dsts))[:ENG])


def rank_program(g, core, T, topo):
    cores = list(T.cores)
    plan = _plan(T, topo)
    rank = T.rank_of(core)
    sem = T.sem

    def send(src, name, rsem, dsts, mask):
        g.remote_dma_fused([_copy(topo, T, src, name, rsem, dsts, mask)], local_sem=sem.sent)

    if rank is None:
        left = 0
        for s, p in enumerate(plan):
            if p["raw"] and p["raw"][0] == core:
                nxt = [cores[p["raw"][1]]]
                mk = _off_chip_mask(topo, core, nxt)
                g.wait_ge(sem.hk, ENG)
                send(T.rl_k[:], "rk", sem.ark, nxt, mk)
                g.wait_ge(sem.hv, ENG)
                send(T.rl_v[:], "rv", sem.arv, nxt, mk)
                left += 2 * ENG
            for h, r in p["srel"]:
                if h == core:
                    dst = [cores[r]]
                    g.wait_ge(sem.hs, ENG)
                    send(T.relay[:], "land%d" % s, sem["arr%d" % s], dst, _off_chip_mask(topo, core, dst))
                    left += ENG
        if left:
            g.wait_ge(sem.sent, left)
        return

    p = plan[rank]
    direct, raw, srel = p["direct"], p["raw"], p["srel"]
    sends = bool(direct or srel)

    if raw:
        g.sync.dma_start(T.k_s[:], T.k[:]).then_inc(sem.ld_k, 16)
    if sends:
        g.sync.dma_start(T.kt_s[:], T.kt[:]).then_inc(sem.ld_kt, 16)
    g.scalar.dma_start(T.v_s[:], T.v[:]).then_inc(sem.ld_v, 16)
    if not raw:
        g.sync.dma_start(T.k_s[:], T.k[:]).then_inc(sem.ld_k, 16)
    g.scalar.dma_start(T.q_s[:], T.q[:]).then_inc(sem.ld_q, 16)
    g.sync.dma_start(T.m_s[:], T.m[:]).then_inc(sem.ld_m, 16)

    ps_s, ps_a, ps_r = T.ps_s[:, 0:P], T.ps_a[:, 0:P], T.ps_r[:, 0:P]

    g.tensor.wait_ge(sem.ld_v, 16)
    if sends:
        g.tensor.wait_ge(sem.ld_kt, 16)
        g.tensor.matmul(ps_s, T.kt_s[:], T.v_s[:], True, True).then_inc(sem.mm_s, 1)
        g.vector.wait_ge(sem.mm_s, 1)
        g.vector.tensor_copy(T.s_b[:], ps_s).then_inc(sem.cp_s, 1)

    left = 0
    if sends:
        hi, lo = _on_chip_masks(topo, cores, core, srel[0][0])
        if raw:
            g.wait_ge(sem.ld_k, 16)
            send(T.k_s[:], "rl_k", sem.hk, [raw[0]], hi)
            left += ENG
        g.wait_ge(sem.cp_s, 1)
        feeds = [_copy(topo, T, T.s_b[:], "relay", sem.hs, [srel[0][0]], hi)]
        if srel[1:]:
            feeds.append(_copy(topo, T, T.s_b[:], "relay", sem.hs, [h for h, _ in srel[1:]], lo))
        g.remote_dma_fused(feeds, local_sem=sem.sent)
        left += ENG * len(feeds)
        if raw:
            g.wait_ge(sem.ld_v, 16)
            send(T.v_s[:], "rl_v", sem.hv, [raw[0]], hi)
            left += ENG
        if direct:
            dst = [cores[r] for r in direct]
            send(T.s_b[:], "land%d" % rank, sem["arr%d" % rank], dst, _off_chip_mask(topo, core, dst))
            left += ENG
        g.wait_ge(sem.sent, left)

    g.tensor.wait_ge(sem.ld_k, 16)
    g.tensor.wait_ge(sem.ld_q, 16)
    g.tensor.matmul(ps_a, T.k_s[:], T.q_s[:], True, True).then_inc(sem.mm_a, 1)
    g.vector.wait_ge(sem.mm_a, 1)
    g.vector.wait_ge(sem.ld_m, 16)
    g.vector.tensor_tensor(T.am_b[:], ps_a, T.m_s[:], AluOpType.mult).then_inc(sem.cp_a, 1)
    g.tensor.wait_ge(sem.cp_a, 1)

    came = []
    for s in range(rank):
        ps = plan[s]
        if rank in ps["direct"]:
            came.append((ps["direct"].index(rank), "S", s))
        if ps["raw"] and ps["raw"][1] == rank:
            came.append((102, "K", s))
            came.append((103.5, "V", s))
        for i, (h, r) in enumerate(ps["srel"]):
            if r == rank:
                came.append(((102.5 if not ps["raw"] else (103, 102.7, 103.2)[i]), "S", s))
    came.sort()
    n_y = sum(1 for e in came if e[1] != "K")

    def ymm(lhsT, rhs, start, stop):
        a = g.tensor.matmul(T.ps_y0[:, 0:H], lhsT, rhs[:, 0:H], start, stop)
        b = g.tensor.matmul(T.ps_y1[:, 0:H], lhsT, rhs[:, H:P], start, stop)
        if stop:
            a.then_inc(sem.mm_y0, 1)
            b.then_inc(sem.mm_y1, 1)

    ymm(T.v_s[:], T.am_b, True, n_y == 0)
    done = 0
    for _, kind, s in came:
        if kind == "K":
            g.tensor.wait_ge(sem.ark, ENG)
            g.tensor.matmul(ps_r, T.rk[:], T.q_s[:], True, True).then_inc(sem.mm_r, 1)
            g.vector.wait_ge(sem.mm_r, 1)
            g.vector.tensor_copy(T.ar_b[:], ps_r).then_inc(sem.cp_r, 1)
            continue
        done += 1
        if kind == "V":
            g.tensor.wait_ge(sem.cp_r, 1)
            g.tensor.wait_ge(sem.arv, ENG)
            ymm(T.rv[:], T.ar_b, False, done == n_y)
        else:
            g.tensor.wait_ge(sem["arr%d" % s], ENG)
            ymm(T["land%d" % s][:], T.q_s, False, done == n_y)

    g.scalar.wait_ge(sem.mm_y0, 1)
    g.scalar.activation(T.y_b[:, 0:H], T.ps_y0[:, 0:H], ActivationFunctionType.Copy).then_inc(sem.cp_y0, 1)
    g.vector.wait_ge(sem.mm_y1, 1)
    g.vector.tensor_copy(T.y_b[:, H:P], T.ps_y1[:, 0:H]).then_inc(sem.cp_y1, 1)
    g.sync.wait_ge(sem.cp_y0, 1)
    g.sync.wait_ge(sem.cp_y1, 1)
    g.sync.dma_start(T.y[:], T.y_b[:]).then_inc(sem.st_y, 16)
    g.sync.wait_ge(sem.st_y, 16)
